import numpy as np, ml_dtypes
CORES = [8,136,40,168]
N = 4
import mx_ref
NC, KT, G, WT = 256, 1, 4, 1
C = np.float32(0.043)
BF = ml_dtypes.bfloat16
def cut(t, i, w=512):
    return t[:, w * i:w * i + w]
def tile(rs):
    return np.stack(rs, axis=2).reshape(128, -1).astype(BF)
def layer(w, X):
    out = []
    for i in range(G):
        for t in range(len(X)):
            p = mx_ref.matmul(mx_ref.quantize(cut(w, len(X) * i + t)), X[t])
            z = p if t == 0 else z + p
        out.append(z)
    return out
def act(Z):
    return [np.maximum(z, 0) * C for z in Z]
def setup_inputs(rng):
    def f(*shape):
        return mx_ref.flush((rng.standard_normal(shape, dtype=np.float32) * np.exp2(rng.integers(-2, 3, shape[:-1] + (1,)))).astype(BF))
    return {"x": f(N, 128, KT * 4 * NC), "w1": f(N, 128, G * KT * 512), "w2": f(N, 128, WT * 512)}
def setup_inputs_blocks(rng):
    d = setup_inputs(rng)
    for k in ("x", "w1", "w2"): d[k] = mx_ref.spread(d[k], rng, 4)
    return d
def setup_inputs_wide(rng):
    d = setup_inputs(rng)
    for k in ("x", "w1", "w2"): d[k] = mx_ref.flush((d[k].astype(np.float32) * np.exp2(rng.integers(-8, 9, (N, 1, 1))).astype(np.float32)).astype(BF))
    return d
def setup_inputs_zeros(rng):
    d = setup_inputs(rng); v = d["x"].reshape(N, 128, -1, 4).copy()
    v[np.broadcast_to((rng.random((N, 1, v.shape[2], 1)) < 0.33), v.shape)] = 0
    d["x"] = v.reshape(d["x"].shape)
    return d
def reference(x, w1, w2):
    H = [mx_ref.quantize(tile(act(layer(w1[j], [mx_ref.quantize(cut(x[j], t, 4 * NC)) for t in range(KT)])))) for j in range(N)]
    y = np.zeros((N, 128, N * WT * NC), np.float32)
    for r in range(N):
        for i in range(WT):
            qw = mx_ref.quantize(cut(w2[r], i))
            for j in range(N):
                y[r][:, NC * (WT * j + i):NC * (WT * j + i) + NC] = mx_ref.matmul(qw, H[j])
    return {"y": y}

@@ -1,0 +1,181 @@
+from concourse.bass import DstId, RemoteDMATransfer
+from concourse.mybir import dt, AluOpType, ActivationFunctionType
+
+NCOL = 256
+HALF = 128
+BANK = 512
+F8 = "float8_e4m3fn_x4"
+
+SCRATCH = {
+    "xb": ("sbuf", [128, 4 * NCOL], "bfloat16"),
+    "w1b": ("sbuf", [128, 2048], "bfloat16"),
+    "w2b": ("sbuf", [128, 512], "bfloat16"),
+    "hb": ("sbuf", [128, 4 * NCOL], "bfloat16"),
+    "qx": ("sbuf", [128, NCOL], F8), "sx": ("sbuf", [128, NCOL], "uint8"),
+    "qw": ("sbuf", [128, 512], F8), "sw": ("sbuf", [128, 512], "uint8"),
+    "qv": ("sbuf", [128, 128], F8), "sv": ("sbuf", [128, 128], "uint8"),
+    "qh": ("sbuf", [128, NCOL], F8), "sh": ("sbuf", [128, NCOL], "uint8"),
+    "cX": ("sbuf", [128, NCOL], F8), "sX": ("sbuf", [128, NCOL], "uint8"),
+    "cP": ("sbuf", [128, NCOL], F8), "sP": ("sbuf", [128, NCOL], "uint8"),
+    "cD": ("sbuf", [128, NCOL], F8), "sD": ("sbuf", [128, NCOL], "uint8"),
+    "yo": ("sbuf", [128, 4 * NCOL], "float32"),
+    "ps": ("psum", [128, 8 * BANK], "float32"),
+}
+SEMAPHORES = (["lxA", "lxB", "lwa", "lwb", "lv", "qxA", "qxB", "qw0", "qw1", "qw2", "qw3", "qv"]
+              + ["z%s%d" % (h, i) for h in "AB" for i in range(4)]
+              + ["actA", "actB", "hA", "hB", "rXA", "rXB", "rP", "rS", "rDA", "rDB", "sent"]
+              + ["m%d" % i for i in range(5)] + ["c%d" % i for i in range(5)] + ["stored"])
+
+
+def rank_program(g, core, T, topo):
+    rank = T.rank_of(core)
+    if rank is None:
+        return
+    s = T.sem
+    cores = list(T.cores)
+    P = [c for c in cores if c != core and topo.host(c) == topo.host(core)][0]
+    X = [c for c in cores if topo.host(c) != topo.host(core) and topo.chip(c) == topo.chip(core)][0]
+    D = [c for c in cores if c not in (core, P, X)][0]
+    ts, v, sc, sy = g.tensor, g.vector, g.scalar, g.sync
+    A, B = slice(0, HALF), slice(HALF, NCOL)
+
+    sy.dma_start(T.xb[:, 0:512], T.x[:, 0:512]).then_inc(s.lxA, 16)
+    sc.dma_start(T.w1b[:, 0:1536], T.w1[:, 0:1536]).then_inc(s.lwa, 16)
+    sy.dma_start(T.w1b[:, 1536:2048], T.w1[:, 1536:2048]).then_inc(s.lwb, 16)
+    sy.dma_start(T.xb[:, 512:1024], T.x[:, 512:1024]).then_inc(s.lxB, 16)
+    sy.dma_start(T.w2b[:], T.w2[:]).then_inc(s.lv, 16)
+
+    v.wait_ge(s.lxA, 16)
+    v.quantize_mx(T.qx[:, A], T.sx[:, A], T.xb[:, 0:512]).then_inc(s.qxA, 1)
+    for i in range(4):
+        if i == 0:
+            v.wait_ge(s.lwa, 16)
+        if i == 3:
+            v.wait_ge(s.lwb, 16)
+        w = slice(128 * i, 128 * i + 128)
+        v.quantize_mx(T.qw[:, w], T.sw[:, w], T.w1b[:, 512 * i:512 * i + 512]).then_inc(s["qw%d" % i], 1)
+
+    def first(h, i, bank):
+        w, c = slice(128 * i, 128 * i + 128), (A if h == "A" else B)
+        ts.matmul_mx(T.ps[:, BANK * bank:BANK * bank + HALF], T.qw[:, w], T.sw[:, w], T.qx[:, c], T.sx[:, c],
+                     True, True).then_inc(s["z%s%d" % (h, i)], 1)
+
+    ts.wait_ge(s.qxA, 1)
+    for i in range(4):
+        ts.wait_ge(s["qw%d" % i], 1)
+        first("A", i, i)
+    ts.wait_ge(s.qxB, 1)
+    for i in range(4):
+        first("B", i, 4 + i)
+
+    def act_scalar(h, i, bank, off):
+        sc.wait_ge(s["z%s%d" % (h, i)], 1)
+        sc.activation(T.hb[:, off + i:off + 512:4], T.ps[:, BANK * bank:BANK * bank + HALF],
+                      ActivationFunctionType.Relu, scale=0.043).then_inc(s["act" + h], 1)
+
+    def act_vector(h, i, bank, off):
+        v.wait_ge(s["z%s%d" % (h, i)], 1)
+        v.tensor_scalar(T.hb[:, off + i:off + 512:4], T.ps[:, BANK * bank:BANK * bank + HALF], 0.0, 0.043,
+                        AluOpType.max, AluOpType.mult).then_inc(s["act" + h], 1)
+
+    for i in range(4):
+        act_scalar("A", i, i, 0)
+    v.wait_ge(s.actA, 4)
+    v.quantize_mx(T.qh[:, A], T.sh[:, A], T.hb[:, 0:512]).then_inc(s.hA, 1)
+    v.wait_ge(s.lxB, 16)
+    v.quantize_mx(T.qx[:, B], T.sx[:, B], T.xb[:, 512:1024]).then_inc(s.qxB, 1)
+    act_scalar("B", 0, 4, 512)
+    act_vector("B", 1, 5, 512)
+    act_scalar("B", 2, 6, 512)
+    act_vector("B", 3, 7, 512)
+    v.wait_ge(s.actB, 4)
+    v.quantize_mx(T.qh[:, B], T.sh[:, B], T.hb[:, 512:1024]).then_inc(s.hB, 1)
+    v.wait_ge(s.lv, 16)
+    v.quantize_mx(T.qv[:], T.sv[:], T.w2b[:]).then_inc(s.qv, 1)
+
+    left = [0]
+
+    def engines(mask):
+        return bin(mask).count("1")
+
+    def mask3(c):
+        m = -1
+        for d in cores:
+            if d != c:
+                m &= topo.mask(c, d)
+        return m
+
+    def send_codes(dst, out, src, cols, sem):
+        rid, pid = topo.addr(dst, core)
+        m = topo.mask(core, dst)
+        g.remote_dma(out[:, cols].bitcast(dt.uint8), src[:, cols].bitcast(dt.uint8), sem, s.sent, pid, rid, m)
+        left[0] += engines(m)
+
+    ids = []
+    for d in (X, P, D):
+        rid, pid = topo.addr(d, core)
+        ids.append(DstId(rid=rid, pnc=pid))
+    nX, nP = engines(topo.mask(X, core)), engines(topo.mask(P, core))
+    nS = sum(engines(mask3(c)) for c in (X, P, D))
+
+    g.wait_ge(s.hA, 1)
+    send_codes(X, T.cX, T.qh, A, s.rXA)
+    g.wait_ge(s.hB, 1)
+    send_codes(X, T.cX, T.qh, B, s.rXB)
+    g.remote_dma_fused([RemoteDMATransfer(dst_ids=ids, dma_engine_mask=mask3(core), remote_sem=s.rS, srcs=[T.sh[:]],
+                                          dsts=[T.sX[:], T.sP[:], T.sD[:]])], local_sem=s.sent)
+    left[0] += engines(mask3(core))
+    send_codes(P, T.cP, T.qh, slice(0, NCOL), s.rP)
+    g.wait_ge(s.rXA, nX)
+    send_codes(P, T.cD, T.cX, A, s.rDA)
+    g.wait_ge(s.rXB, nX)
+    send_codes(P, T.cD, T.cX, B, s.rDB)
+    g.wait_ge(s.sent, left[0])
+
+    def second(k, codes, scales, cols, bank):
+        n = cols.stop - cols.start
+        ts.matmul_mx(T.ps[:, BANK * bank:BANK * bank + n], T.qv[:], T.sv[:], codes[:, cols], scales[:, cols],
+                     True, True).then_inc(s["m%d" % k], 1)
+
+    def copy_scalar(k, bank, col, n):
+        sc.wait_ge(s["m%d" % k], 1)
+        sc.activation(T.yo[:, col:col + n], T.ps[:, BANK * bank:BANK * bank + n],
+                      ActivationFunctionType.Copy).then_inc(s["c%d" % k], 1)
+
+    def copy_vector(k, bank, col, n):
+        v.wait_ge(s["m%d" % k], 1)
+        v.tensor_copy(T.yo[:, col:col + n], T.ps[:, BANK * bank:BANK * bank + n]).then_inc(s["c%d" % k], 1)
+
+    def store(k, col, n):
+        sy.wait_ge(s["c%d" % k], 1)
+        sy.dma_start(T.y[:, col:col + n], T.yo[:, col:col + n]).then_inc(s.stored, 16)
+
+    full = slice(0, NCOL)
+    y0, yX, yP, yD = [NCOL * T.rank_of(c) for c in (core, X, P, D)]
+    ts.wait_ge(s.hB, 1)
+    ts.wait_ge(s.qv, 1)
+    second(0, T.qh, T.sh, full, 0)
+    ts.wait_ge(s.rXA, nX)
+    ts.wait_ge(s.rXB, nX)
+    ts.wait_ge(s.rS, nS)
+    second(1, T.cX, T.sX, full, 1)
+    ts.wait_ge(s.rP, nP)
+    second(2, T.cP, T.sP, full, 2)
+    ts.wait_ge(s.rDA, nP)
+    second(3, T.cD, T.sD, A, 3)
+    ts.wait_ge(s.rDB, nP)
+    second(4, T.cD, T.sD, B, 4)
+
+    copy_scalar(0, 0, y0, NCOL)
+    copy_vector(1, 1, yX, NCOL)
+    copy_scalar(2, 2, yP, NCOL)
+    copy_scalar(3, 3, yD, HALF)
+    copy_vector(4, 4, yD + HALF, HALF)
+
+    sy.wait_ge(s.rXB, nX)
+    store(0, y0, NCOL)
+    store(1, yX, NCOL)
+    store(2, yP, NCOL)
+    store(3, yD, HALF)
+    store(4, yD + HALF, HALF)
+    sy.wait_ge(s.stored, 16 * 5)

@@ -1,6 +1,7 @@
 from concourse.bass import DstId, RemoteDMATransfer
 from concourse.mybir import dt, AluOpType, ActivationFunctionType
 
+WORLD = 256
 NCOL = 256
 HALF = 128
 BANK = 512
@@ -23,21 +24,70 @@ SCRATCH = {
 }
 SEMAPHORES = (["lxA", "lxB", "lwa", "lwb", "lv", "qxA", "qxB", "qw0", "qw1", "qw2", "qw3", "qv"]
               + ["z%s%d" % (h, i) for h in "AB" for i in range(4)]
-              + ["actA", "actB", "hA", "hB", "rXA", "rXB", "rP", "rS", "rDA", "rDB", "sent"]
-              + ["m%d" % i for i in range(5)] + ["c%d" % i for i in range(5)] + ["stored"])
+              + ["actA", "actB", "hA", "hB", "rXA", "rXB", "rPA", "rPB", "rS", "rDA", "rDB", "sent", "helpA", "helpB"]
+              + ["m%d" % i for i in range(6)] + ["c%d" % i for i in range(6)] + ["stored"])
+A, B = slice(0, HALF), slice(HALF, NCOL)
+
+
+def engines(mask):
+    return bin(mask).count("1")
+
+
+def roles(core, cores, topo):
+    P = [c for c in cores if c != core and topo.host(c) == topo.host(core)][0]
+    X = [c for c in cores if topo.host(c) != topo.host(core) and topo.chip(c) == topo.chip(core)][0]
+    D = [c for c in cores if c not in (core, P, X)][0]
+    H = [c for c in range(WORLD) if (topo.host(c), topo.chip(c)) == (topo.host(core), topo.chip(core))
+         and topo.die(c) != topo.die(core)][0]
+    return P, X, D, H
+
+
+def inner(topo, rank_core, helper, other):
+    return topo.mask(rank_core, helper) & ~topo.mask(rank_core, other)
+
+
+def sender(g, core, T, topo):
+    left = [0]
+
+    def send(*transfers):
+        out = []
+        for src, dsts, sem, mask in transfers:
+            ids = []
+            for d, _ in dsts:
+                rid, pid = topo.addr(d, core)
+                ids.append(DstId(rid=rid, pnc=pid))
+            out.append(RemoteDMATransfer(dst_ids=ids, dma_engine_mask=mask, remote_sem=sem, srcs=[src],
+                                         dsts=[o for _, o in dsts]))
+            left[0] += engines(mask)
+        g.remote_dma_fused(out, local_sem=T.sem.sent)
+
+    return send, left
+
+
+def code_bytes(t, cols):
+    return t[:, cols].bitcast(dt.uint8)
+
+
+def helper_program(g, core, T, topo):
+    for r in T.cores:
+        P, X, D, H = roles(r, list(T.cores), topo)
+        if core == H:
+            send, left = sender(g, core, T, topo)
+            for h, cols in (("A", A), ("B", B)):
+                g.wait_ge(T.sem["help" + h], engines(inner(topo, r, core, X)))
+                send((code_bytes(T.qh, cols), [(P, code_bytes(T.cP, cols))], T.sem["rP" + h], topo.mask(core, P)))
+            g.wait_ge(T.sem.sent, left[0])
 
 
 def rank_program(g, core, T, topo):
     rank = T.rank_of(core)
     if rank is None:
+        helper_program(g, core, T, topo)
         return
     s = T.sem
     cores = list(T.cores)
-    P = [c for c in cores if c != core and topo.host(c) == topo.host(core)][0]
-    X = [c for c in cores if topo.host(c) != topo.host(core) and topo.chip(c) == topo.chip(core)][0]
-    D = [c for c in cores if c not in (core, P, X)][0]
+    P, X, D, H = roles(core, cores, topo)
     ts, v, sc, sy = g.tensor, g.vector, g.scalar, g.sync
-    A, B = slice(0, HALF), slice(HALF, NCOL)
 
     sy.dma_start(T.xb[:, 0:512], T.x[:, 0:512]).then_inc(s.lxA, 16)
     sc.dma_start(T.w1b[:, 0:1536], T.w1[:, 0:1536]).then_inc(s.lwa, 16)
@@ -93,11 +143,6 @@ def rank_program(g, core, T, topo):
     v.wait_ge(s.lv, 16)
     v.quantize_mx(T.qv[:], T.sv[:], T.w2b[:]).then_inc(s.qv, 1)
 
-    left = [0]
-
-    def engines(mask):
-        return bin(mask).count("1")
-
     def mask3(c):
         m = -1
         for d in cores:
@@ -105,77 +150,72 @@ def rank_program(g, core, T, topo):
                 m &= topo.mask(c, d)
         return m
 
-    def send_codes(dst, out, src, cols, sem):
-        rid, pid = topo.addr(dst, core)
-        m = topo.mask(core, dst)
-        g.remote_dma(out[:, cols].bitcast(dt.uint8), src[:, cols].bitcast(dt.uint8), sem, s.sent, pid, rid, m)
-        left[0] += engines(m)
-
-    ids = []
-    for d in (X, P, D):
-        rid, pid = topo.addr(d, core)
-        ids.append(DstId(rid=rid, pnc=pid))
-    nX, nP = engines(topo.mask(X, core)), engines(topo.mask(P, core))
+    send, left = sender(g, core, T, topo)
+    toX, toP, toH = topo.mask(core, X), topo.mask(core, P), inner(topo, core, H, X)
+    nX, nD = engines(topo.mask(X, core)), engines(topo.mask(P, core))
+    nP = engines(topo.mask(roles(P, cores, topo)[3], core))
     nS = sum(engines(mask3(c)) for c in (X, P, D))
-
+    hA, hB = code_bytes(T.qh, A), code_bytes(T.qh, B)
     g.wait_ge(s.hA, 1)
-    send_codes(X, T.cX, T.qh, A, s.rXA)
+    send((hA, [(X, code_bytes(T.cX, A))], s.rXA, toX))
+    send((hA, [(H, hA)], s.helpA, toH))
     g.wait_ge(s.hB, 1)
-    send_codes(X, T.cX, T.qh, B, s.rXB)
-    g.remote_dma_fused([RemoteDMATransfer(dst_ids=ids, dma_engine_mask=mask3(core), remote_sem=s.rS, srcs=[T.sh[:]],
-                                          dsts=[T.sX[:], T.sP[:], T.sD[:]])], local_sem=s.sent)
-    left[0] += engines(mask3(core))
-    send_codes(P, T.cP, T.qh, slice(0, NCOL), s.rP)
-    g.wait_ge(s.rXA, nX)
-    send_codes(P, T.cD, T.cX, A, s.rDA)
-    g.wait_ge(s.rXB, nX)
-    send_codes(P, T.cD, T.cX, B, s.rDB)
+    send((hB, [(X, code_bytes(T.cX, B))], s.rXB, toX),
+         (hB, [(H, hB)], s.helpB, toH))
+    send((T.sh[:], [(X, T.sX[:]), (P, T.sP[:]), (D, T.sD[:])], s.rS, mask3(core)))
+    for h, cols in (("A", A), ("B", B)):
+        g.wait_ge(s["rX" + h], nX)
+        send((code_bytes(T.cX, cols), [(P, code_bytes(T.cD, cols))], s["rD" + h], toP))
     g.wait_ge(s.sent, left[0])
 
-    def second(k, codes, scales, cols, bank):
+    def second(k, qt, st, cols):
         n = cols.stop - cols.start
-        ts.matmul_mx(T.ps[:, BANK * bank:BANK * bank + n], T.qv[:], T.sv[:], codes[:, cols], scales[:, cols],
+        ts.matmul_mx(T.ps[:, BANK * k:BANK * k + n], T.qv[:], T.sv[:], qt[:, cols], st[:, cols],
                      True, True).then_inc(s["m%d" % k], 1)
 
-    def copy_scalar(k, bank, col, n):
+    def copy_scalar(k, col, n):
         sc.wait_ge(s["m%d" % k], 1)
-        sc.activation(T.yo[:, col:col + n], T.ps[:, BANK * bank:BANK * bank + n],
+        sc.activation(T.yo[:, col:col + n], T.ps[:, BANK * k:BANK * k + n],
                       ActivationFunctionType.Copy).then_inc(s["c%d" % k], 1)
 
-    def copy_vector(k, bank, col, n):
+    def copy_vector(k, col, n):
         v.wait_ge(s["m%d" % k], 1)
-        v.tensor_copy(T.yo[:, col:col + n], T.ps[:, BANK * bank:BANK * bank + n]).then_inc(s["c%d" % k], 1)
+        v.tensor_copy(T.yo[:, col:col + n], T.ps[:, BANK * k:BANK * k + n]).then_inc(s["c%d" % k], 1)
 
-    def store(k, col, n):
-        sy.wait_ge(s["c%d" % k], 1)
-        sy.dma_start(T.y[:, col:col + n], T.yo[:, col:col + n]).then_inc(s.stored, 16)
+    def store(queue, k, col, n):
+        queue.wait_ge(s["c%d" % k], 1)
+        queue.dma_start(T.y[:, col:col + n], T.yo[:, col:col + n]).then_inc(s.stored, 16)
 
     full = slice(0, NCOL)
     y0, yX, yP, yD = [NCOL * T.rank_of(c) for c in (core, X, P, D)]
     ts.wait_ge(s.hB, 1)
     ts.wait_ge(s.qv, 1)
-    second(0, T.qh, T.sh, full, 0)
+    second(0, T.qh, T.sh, full)
     ts.wait_ge(s.rXA, nX)
     ts.wait_ge(s.rXB, nX)
     ts.wait_ge(s.rS, nS)
-    second(1, T.cX, T.sX, full, 1)
-    ts.wait_ge(s.rP, nP)
-    second(2, T.cP, T.sP, full, 2)
-    ts.wait_ge(s.rDA, nP)
-    second(3, T.cD, T.sD, A, 3)
-    ts.wait_ge(s.rDB, nP)
-    second(4, T.cD, T.sD, B, 4)
+    second(1, T.cX, T.sX, full)
+    ts.wait_ge(s.rDA, nD)
+    second(3, T.cD, T.sD, A)
+    ts.wait_ge(s.rPA, nP)
+    second(5, T.cP, T.sP, A)
+    ts.wait_ge(s.rDB, nD)
+    second(4, T.cD, T.sD, B)
+    ts.wait_ge(s.rPB, nP)
+    second(2, T.cP, T.sP, B)
 
-    copy_scalar(0, 0, y0, NCOL)
-    copy_vector(1, 1, yX, NCOL)
-    copy_scalar(2, 2, yP, NCOL)
-    copy_scalar(3, 3, yD, HALF)
-    copy_vector(4, 4, yD + HALF, HALF)
+    copy_scalar(0, y0, NCOL)
+    copy_vector(1, yX, NCOL)
+    copy_vector(3, yD, HALF)
+    copy_scalar(5, yP, HALF)
+    copy_vector(4, yD + HALF, HALF)
+    store(sc, 5, yP, HALF)
+    copy_scalar(2, yP + HALF, HALF)
+    store(sc, 2, yP + HALF, HALF)
 
-    sy.wait_ge(s.rXB, nX)
-    store(0, y0, NCOL)
-    store(1, yX, NCOL)
-    store(2, yP, NCOL)
-    store(3, yD, HALF)
-    store(4, yD + HALF, HALF)
-    sy.wait_ge(s.stored, 16 * 5)
+    store(sy, 0, y0, NCOL)
+    store(sy, 1, yX, NCOL)
+    store(sy, 3, yD, HALF)
+    store(sy, 4, yD + HALF, HALF)
+    sy.wait_ge(s.c2, 1)
+    sy.wait_ge(s.stored, 16 * 6)

from concourse.bass import DstId, RemoteDMATransfer
from concourse.mybir import dt, AluOpType, ActivationFunctionType

WORLD = 256
NCOL = 256
HALF = 128
BANK = 512
F8 = "float8_e4m3fn_x4"

SCRATCH = {
    "xb": ("sbuf", [128, 4 * NCOL], "bfloat16"),
    "w1b": ("sbuf", [128, 2048], "bfloat16"),
    "w2b": ("sbuf", [128, 512], "bfloat16"),
    "hb": ("sbuf", [128, 4 * NCOL], "bfloat16"),
    "qx": ("sbuf", [128, NCOL], F8), "sx": ("sbuf", [128, NCOL], "uint8"),
    "qw": ("sbuf", [128, 512], F8), "sw": ("sbuf", [128, 512], "uint8"),
    "qv": ("sbuf", [128, 128], F8), "sv": ("sbuf", [128, 128], "uint8"),
    "qh": ("sbuf", [128, NCOL], F8), "sh": ("sbuf", [128, NCOL], "uint8"),
    "cX": ("sbuf", [128, NCOL], F8), "sX": ("sbuf", [128, NCOL], "uint8"),
    "cP": ("sbuf", [128, NCOL], F8), "sP": ("sbuf", [128, NCOL], "uint8"),
    "cD": ("sbuf", [128, NCOL], F8), "sD": ("sbuf", [128, NCOL], "uint8"),
    "yo": ("sbuf", [128, 4 * NCOL], "float32"),
    "ps": ("psum", [128, 8 * BANK], "float32"),
}
SEMAPHORES = (["lxA", "lxB", "lwa", "lwb", "lv", "qxA", "qxB", "qw0", "qw1", "qw2", "qw3", "qv"]
              + ["z%s%d" % (h, i) for h in "AB" for i in range(4)]
              + ["actA", "actB", "hA", "hB", "rXA", "rXB", "rPA", "rPB", "rS", "rDA", "rDB", "sent", "helpA", "helpB"]
              + ["m%d" % i for i in range(6)] + ["c%d" % i for i in range(6)] + ["stored"])
A, B = slice(0, HALF), slice(HALF, NCOL)


def engines(mask):
    return bin(mask).count("1")


def roles(core, cores, topo):
    P = [c for c in cores if c != core and topo.host(c) == topo.host(core)][0]
    X = [c for c in cores if topo.host(c) != topo.host(core) and topo.chip(c) == topo.chip(core)][0]
    D = [c for c in cores if c not in (core, P, X)][0]
    H = [c for c in range(WORLD) if (topo.host(c), topo.chip(c)) == (topo.host(core), topo.chip(core))
         and topo.die(c) != topo.die(core)][0]
    return P, X, D, H


def inner(topo, rank_core, helper, other):
    return topo.mask(rank_core, helper) & ~topo.mask(rank_core, other)


def sender(g, core, T, topo):
    left = [0]

    def send(*transfers):
        out = []
        for src, dsts, sem, mask in transfers:
            ids = []
            for d, _ in dsts:
                rid, pid = topo.addr(d, core)
                ids.append(DstId(rid=rid, pnc=pid))
            out.append(RemoteDMATransfer(dst_ids=ids, dma_engine_mask=mask, remote_sem=sem, srcs=[src],
                                         dsts=[o for _, o in dsts]))
            left[0] += engines(mask)
        g.remote_dma_fused(out, local_sem=T.sem.sent)

    return send, left


def code_bytes(t, cols):
    return t[:, cols].bitcast(dt.uint8)


def helper_program(g, core, T, topo):
    for r in T.cores:
        P, X, D, H = roles(r, list(T.cores), topo)
        if core == H:
            send, left = sender(g, core, T, topo)
            for h, cols in (("A", A), ("B", B)):
                g.wait_ge(T.sem["help" + h], engines(inner(topo, r, core, X)))
                send((code_bytes(T.qh, cols), [(P, code_bytes(T.cP, cols))], T.sem["rP" + h], topo.mask(core, P)))
            g.wait_ge(T.sem.sent, left[0])


def rank_program(g, core, T, topo):
    rank = T.rank_of(core)
    if rank is None:
        helper_program(g, core, T, topo)
        return
    s = T.sem
    cores = list(T.cores)
    P, X, D, H = roles(core, cores, topo)
    ts, v, sc, sy = g.tensor, g.vector, g.scalar, g.sync

    sy.dma_start(T.xb[:, 0:512], T.x[:, 0:512]).then_inc(s.lxA, 16)
    sc.dma_start(T.w1b[:, 0:1536], T.w1[:, 0:1536]).then_inc(s.lwa, 16)
    sy.dma_start(T.w1b[:, 1536:2048], T.w1[:, 1536:2048]).then_inc(s.lwb, 16)
    sy.dma_start(T.xb[:, 512:1024], T.x[:, 512:1024]).then_inc(s.lxB, 16)
    sy.dma_start(T.w2b[:], T.w2[:]).then_inc(s.lv, 16)

    v.wait_ge(s.lxA, 16)
    v.quantize_mx(T.qx[:, A], T.sx[:, A], T.xb[:, 0:512]).then_inc(s.qxA, 1)
    for i in range(4):
        if i == 0:
            v.wait_ge(s.lwa, 16)
        if i == 3:
            v.wait_ge(s.lwb, 16)
        w = slice(128 * i, 128 * i + 128)
        v.quantize_mx(T.qw[:, w], T.sw[:, w], T.w1b[:, 512 * i:512 * i + 512]).then_inc(s["qw%d" % i], 1)

    def first(h, i, bank):
        w, c = slice(128 * i, 128 * i + 128), (A if h == "A" else B)
        ts.matmul_mx(T.ps[:, BANK * bank:BANK * bank + HALF], T.qw[:, w], T.sw[:, w], T.qx[:, c], T.sx[:, c],
                     True, True).then_inc(s["z%s%d" % (h, i)], 1)

    ts.wait_ge(s.qxA, 1)
    for i in range(4):
        ts.wait_ge(s["qw%d" % i], 1)
        first("A", i, i)
    ts.wait_ge(s.qxB, 1)
    for i in range(4):
        first("B", i, 4 + i)

    def act_scalar(h, i, bank, off):
        sc.wait_ge(s["z%s%d" % (h, i)], 1)
        sc.activation(T.hb[:, off + i:off + 512:4], T.ps[:, BANK * bank:BANK * bank + HALF],
                      ActivationFunctionType.Relu, scale=0.043).then_inc(s["act" + h], 1)

    def act_vector(h, i, bank, off):
        v.wait_ge(s["z%s%d" % (h, i)], 1)
        v.tensor_scalar(T.hb[:, off + i:off + 512:4], T.ps[:, BANK * bank:BANK * bank + HALF], 0.0, 0.043,
                        AluOpType.max, AluOpType.mult).then_inc(s["act" + h], 1)

    for i in range(4):
        act_scalar("A", i, i, 0)
    v.wait_ge(s.actA, 4)
    v.quantize_mx(T.qh[:, A], T.sh[:, A], T.hb[:, 0:512]).then_inc(s.hA, 1)
    v.wait_ge(s.lxB, 16)
    v.quantize_mx(T.qx[:, B], T.sx[:, B], T.xb[:, 512:1024]).then_inc(s.qxB, 1)
    act_scalar("B", 0, 4, 512)
    act_vector("B", 1, 5, 512)
    act_scalar("B", 2, 6, 512)
    act_vector("B", 3, 7, 512)
    v.wait_ge(s.actB, 4)
    v.quantize_mx(T.qh[:, B], T.sh[:, B], T.hb[:, 512:1024]).then_inc(s.hB, 1)
    v.wait_ge(s.lv, 16)
    v.quantize_mx(T.qv[:], T.sv[:], T.w2b[:]).then_inc(s.qv, 1)

    def mask3(c):
        m = -1
        for d in cores:
            if d != c:
                m &= topo.mask(c, d)
        return m

    send, left = sender(g, core, T, topo)
    toX, toP, toH = topo.mask(core, X), topo.mask(core, P), inner(topo, core, H, X)
    nX, nD = engines(topo.mask(X, core)), engines(topo.mask(P, core))
    nP = engines(topo.mask(roles(P, cores, topo)[3], core))
    nS = sum(engines(mask3(c)) for c in (X, P, D))
    hA, hB = code_bytes(T.qh, A), code_bytes(T.qh, B)
    g.wait_ge(s.hA, 1)
    send((hA, [(X, code_bytes(T.cX, A))], s.rXA, toX))
    send((hA, [(H, hA)], s.helpA, toH))
    g.wait_ge(s.hB, 1)
    send((hB, [(X, code_bytes(T.cX, B))], s.rXB, toX),
         (hB, [(H, hB)], s.helpB, toH))
    send((T.sh[:], [(X, T.sX[:]), (P, T.sP[:]), (D, T.sD[:])], s.rS, mask3(core)))
    for h, cols in (("A", A), ("B", B)):
        g.wait_ge(s["rX" + h], nX)
        send((code_bytes(T.cX, cols), [(P, code_bytes(T.cD, cols))], s["rD" + h], toP))
    g.wait_ge(s.sent, left[0])

    def second(k, qt, st, cols):
        n = cols.stop - cols.start
        ts.matmul_mx(T.ps[:, BANK * k:BANK * k + n], T.qv[:], T.sv[:], qt[:, cols], st[:, cols],
                     True, True).then_inc(s["m%d" % k], 1)

    def copy_scalar(k, col, n):
        sc.wait_ge(s["m%d" % k], 1)
        sc.activation(T.yo[:, col:col + n], T.ps[:, BANK * k:BANK * k + n],
                      ActivationFunctionType.Copy).then_inc(s["c%d" % k], 1)

    def copy_vector(k, col, n):
        v.wait_ge(s["m%d" % k], 1)
        v.tensor_copy(T.yo[:, col:col + n], T.ps[:, BANK * k:BANK * k + n]).then_inc(s["c%d" % k], 1)

    def store(queue, k, col, n):
        queue.wait_ge(s["c%d" % k], 1)
        queue.dma_start(T.y[:, col:col + n], T.yo[:, col:col + n]).then_inc(s.stored, 16)

    full = slice(0, NCOL)
    y0, yX, yP, yD = [NCOL * T.rank_of(c) for c in (core, X, P, D)]
    ts.wait_ge(s.hB, 1)
    ts.wait_ge(s.qv, 1)
    second(0, T.qh, T.sh, full)
    ts.wait_ge(s.rXA, nX)
    ts.wait_ge(s.rXB, nX)
    ts.wait_ge(s.rS, nS)
    second(1, T.cX, T.sX, full)
    ts.wait_ge(s.rDA, nD)
    second(3, T.cD, T.sD, A)
    ts.wait_ge(s.rPA, nP)
    second(5, T.cP, T.sP, A)
    ts.wait_ge(s.rDB, nD)
    second(4, T.cD, T.sD, B)
    ts.wait_ge(s.rPB, nP)
    second(2, T.cP, T.sP, B)

    copy_scalar(0, y0, NCOL)
    copy_vector(1, yX, NCOL)
    copy_vector(3, yD, HALF)
    copy_scalar(5, yP, HALF)
    copy_vector(4, yD + HALF, HALF)
    store(sc, 5, yP, HALF)
    copy_scalar(2, yP + HALF, HALF)
    store(sc, 2, yP + HALF, HALF)

    store(sy, 0, y0, NCOL)
    store(sy, 1, yX, NCOL)
    store(sy, 3, yD, HALF)
    store(sy, 4, yD + HALF, HALF)
    sy.wait_ge(s.c2, 1)
    sy.wait_ge(s.stored, 16 * 6)
